import numpy as np
import ml_dtypes


def mxq(x, axis, fmt="e4m3"):
    dtype, down = {"e4m3": (ml_dtypes.float8_e4m3fn, 7), "e5m2": (ml_dtypes.float8_e5m2, 14)}[fmt]
    v = np.moveaxis(np.asarray(x, np.float32).astype(ml_dtypes.bfloat16).astype(np.float64), axis, -1)
    blocks = v.reshape(v.shape[:-1] + (-1, 32))
    amax = np.abs(blocks).max(-1, keepdims=True)
    byte = np.maximum(np.where(amax > 0, np.frexp(amax)[1] - 1 + 127, 0) - down, 1)
    scale = np.exp2(byte - 127.0)
    codes = (blocks / scale).astype(np.float32).astype(dtype).astype(np.float64)
    return np.moveaxis((codes * scale).reshape(v.shape), -1, axis)


WIDE = False


def mx_kscale(k):
    if not WIDE:
        return np.ones(k)
    levels = np.array([10, -10, 5, -5, 0])
    if k % 512:
        return np.exp2(np.random.permutation(np.resize(levels, k // 32))).repeat(32)
    a = np.empty((k // 512, 16))
    for p in range(k // 512):
        a[p, :8] = np.random.permutation(np.resize(levels, 8))
        for g in range(8):
            far = levels[np.abs(levels - a[p, g]) >= 10]
            a[p, g + 8] = far[np.random.randint(len(far))]
    return np.exp2(a.ravel()).repeat(32)


BF16 = ml_dtypes.bfloat16


def bf(x):
    return np.asarray(x, np.float32).astype(BF16)


def f64(x):
    return np.asarray(x).astype(np.float64)

E4M3FN = np.array([(-1.0 if i & 128 else 1.0) * ((1.0 + (i & 7) / 8.0) * 2.0 ** (((i >> 3) & 15) - 7) if i & 120 else (i & 7) * 2.0 ** -9) for i in range(256)])


def e4m3fn_bytes(y):
    return np.clip(np.asarray(y, np.float64), -448.0, 448.0).astype(np.float32).astype(ml_dtypes.float8_e4m3fn).view(np.uint8)


def e4m3fn_values(b):
    return E4M3FN[b]


T, D, R, B = 4096, 1024, 512, 128


def setup_inputs():
    s, t = mx_kscale(D), mx_kscale(R)
    c = f64(bf(1 + 0.1 * np.random.standard_normal(D)))
    z = np.random.standard_normal((T, D))
    v = np.linalg.svd(np.random.standard_normal((D, D)))[2][:R].T
    d = {"x": bf(z / c * s),
         "g": bf(c / s),
         "a": bf((1 + 0.1 * np.random.standard_normal(R)) * t)}
    for name, w in (("w1", v * (c / s)[:, None]), ("w2", v / t)):
        scale = (np.abs(w).reshape(D // B, B, R // B, B).max(axis=(1, 3)) / 448).astype(np.float32)
        d[name + "_bytes"] = e4m3fn_bytes(w / np.repeat(np.repeat(f64(scale), B, axis=0), B, axis=1))
        d[name + "_scale"] = scale
    return d


def reference(x, g, a, w1_bytes, w1_scale, w2_bytes, w2_scale):
    x = f64(x)
    w1 = e4m3fn_values(w1_bytes) * np.repeat(np.repeat(f64(w1_scale), B, axis=0), B, axis=1)
    w2 = e4m3fn_values(w2_bytes) * np.repeat(np.repeat(f64(w2_scale), B, axis=0), B, axis=1)
    h = (mxq(x, 1, "e4m3") @ mxq(w1, 0, "e4m3")) * f64(a)
    y = mxq(h, 1, "e4m3") @ mxq(w2, 1, "e4m3").T
    e = x * f64(g) - y
    return e * e

@@ -1,0 +1,351 @@
+from contextlib import ExitStack
+
+import concourse.mybir as mybir
+from concourse.masks import make_identity
+
+T, D, R = 4096, 1024, 512
+FLOPS = 4 * T * D * R
+
+F32 = mybir.dt.float32
+BF16 = mybir.dt.bfloat16
+U32 = mybir.dt.uint32
+U8 = mybir.dt.uint8
+E4M3 = mybir.dt.float8_e4m3fn
+X4 = mybir.dt.float8_e4m3fn_x4
+ALU = mybir.AluOpType
+ACT = mybir.ActivationFunctionType
+
+P = 128
+NP = T // 256
+KIND = "DDTDDTDDTDDTDTDD"
+XG = ["GG","GG","GG","GG","GG","GG","GG","GG","GG","GG","GG","GG","GG","GG","GG","GG"]
+
+
+def tile_sensor_residual_squared_d7_kernel(tc, x, g, a, w1_bytes, w1_scale, w2_bytes, w2_scale, out):
+    nc = tc.nc
+    xv = x.rearrange("(b p r) d -> b p (r d)", p=P, r=2)
+    ov = out.rearrange("(b p r) d -> b p r d", p=P, r=2)
+    with ExitStack() as ctx:
+        keep = ctx.enter_context(tc.tile_pool(name="keep", bufs=1))
+        px = ctx.enter_context(tc.tile_pool(name="px", bufs=10))
+        work = ctx.enter_context(tc.tile_pool(name="work", bufs=3))
+        psum = ctx.enter_context(tc.psum_pool(name="psum", bufs=2))
+        ctx.enter_context(tc.manual_schedule())
+
+        X, GX, XC, XS, HB, HG, HC, HS, Y, XGT, O, ET = {}, {}, {}, {}, {}, {}, {}, {}, {}, {}, {}, {}
+
+        def load_x(b):
+            xt = px.tile([P, 2, D], BF16, name="xt", align_bytes=64)
+            nc.sync.dma_start(out=xt[:].rearrange("p r d -> p (r d)"), in_=xv[b])
+            X[b] = xt
+
+        b1 = keep.tile([P, 2, 2048], U8, name="b1", align_bytes=64)
+        b2 = keep.tile([P, 2, 2048], U8, name="b2", align_bytes=64)
+        w1v = w1_bytes.rearrange("(g p t) n -> p g (t n)", p=P, t=4)
+        w2v = w2_bytes.rearrange("(g p t) n -> p g (t n)", p=P, t=4)
+        nc.sync.dma_start(out=b1[:, 0, :], in_=w1v[:, 0, :])
+        load_x(0)
+        nc.sync.dma_start(out=b1[:, 1, :], in_=w1v[:, 1, :])
+        sall = keep.tile([P, 2, 32], F32, name="sall")
+        nc.scalar.dma_start(out=sall[:, 0, :], in_=w1_scale.rearrange("i j -> (i j)").partition_broadcast(P))
+        nc.scalar.dma_start(out=sall[:, 1, :], in_=w2_scale.rearrange("i j -> (i j)").partition_broadcast(P))
+        a4 = keep.tile([P, 4], BF16, name="a4")
+        nc.scalar.dma_start(out=a4[:], in_=a.rearrange("(p t) -> p t", t=4))
+        for h in range(2):
+            nc.sync.dma_start(out=b2[:, h, :], in_=w2v[:, h, :])
+        load_x(1)
+        gb = keep.tile([P, D], BF16, name="gb", align_bytes=64)
+        nc.scalar.dma_start(out=gb[:], in_=g.partition_broadcast(P))
+        gt = keep.tile([P, 2, 4], BF16, name="gt")
+        nc.scalar.dma_start(out=gt[:], in_=g.rearrange("(g p t) -> p g t", p=P, t=4))
+        for b in range(2, 8):
+            load_x(b)
+
+        ident = keep.tile([P, P], F32, name="ident", align_bytes=64)
+        make_identity(nc, ident[:])
+
+        s = keep.tile([P, 2, 2, 4], F32, name="s")
+        for q in range(4):
+            rows = slice(32 * q, 32 * q + 32)
+            nc.vector.tensor_copy(
+                out=s[rows],
+                in_=sall[rows].rearrange("p w (h q j) -> p w h q j", q=4, j=4)[:, :, :, q, :],
+            )
+
+        def transposes(b):
+            GX[b] = work.tile([P, 2, 256, 4], BF16, name="gx", align_bytes=64, bufs=7)
+            for r in range(2):
+                bank = psum.tile([P, 2, 2, P], F32, name="xtb")
+                words = X[b][:, r, :].bitcast(F32)
+                for h in range(2):
+                    for u in range(2):
+                        nc.tensor.transpose(bank[:, h, u, :], words[:, 256 * h + u : 256 * (h + 1) : 2], ident[:])
+                nc.scalar.copy(
+                    out=GX[b][:, :, 128 * r : 128 * r + 128, :].bitcast(F32), in_=bank[:].rearrange("p h u n -> p h n u")
+                )
+
+        def quantize_x(b):
+            XC[b] = work.tile([P, 2, 256], U32, name="xc", align_bytes=64)
+            XS[b] = work.tile([P, 2, 256], U8, name="xs", align_bytes=64)
+            nc.vector.quantize_mx(
+                out=XC[b][:].rearrange("p h n -> p (h n)").bitcast(X4),
+                scales=XS[b][:].rearrange("p h n -> p (h n)"),
+                in_=GX[b][:].rearrange("p h n t -> p (h n t)"),
+            )
+
+        w1c = keep.tile([P, 2, 512], U32, name="w1c", align_bytes=64)
+        w1s = keep.tile([P, 2, 512], U8, name="w1s", align_bytes=64)
+        w2c = keep.tile([P, 2, 512], U32, name="w2c", align_bytes=64)
+        w2s = keep.tile([P, 2, 512], U8, name="w2s", align_bytes=64)
+        wide1 = keep.tile([P, 2, 4, 512], BF16, name="wide1", align_bytes=64)
+        wide2 = keep.tile([P, 2, 4, 512], BF16, name="wide2", align_bytes=64)
+        grp1 = keep.tile([P, 2, 4, P, 4], BF16, name="grp1", align_bytes=64)
+        ws2 = keep.tile([P, 2, 4, 512], BF16, name="ws2", align_bytes=64)
+        grp2 = keep.tile([P, 2, 4, P, 4], BF16, name="grp2", align_bytes=64)
+
+        def widen(eng, wide, byt, h):
+            o_ = wide[:, h, :, :].rearrange("p t n -> p (t n)")
+            i_ = byt[:, h, :].bitcast(E4M3)
+            if eng == "V":
+                nc.vector.tensor_copy(out=o_, in_=i_)
+            elif eng == "G":
+                nc.gpsimd.tensor_copy(out=o_, in_=i_)
+            else:
+                nc.scalar.copy(out=o_, in_=i_)
+
+        def group_w1(eng, h, j):
+            o_ = grp1[:, h, :, 32 * j : 32 * j + 32, :]
+            i_ = wide1[:, h, :, 128 * j : 128 * j + 128].rearrange("p t (m u) -> p u m t", u=4)
+            if eng == "V":
+                nc.vector.tensor_scalar(out=o_, in0=i_, scalar1=s[:, 0, h, j : j + 1], scalar2=None, op0=ALU.mult)
+            else:
+                nc.scalar.activation(out=o_, in_=i_, func=ACT.Copy, scale=s[:, 0, h, j : j + 1])
+
+        def quantize_w(codes, scales, grp, h):
+            nc.vector.quantize_mx(
+                out=codes[:, h, :].bitcast(X4), scales=scales[:, h, :], in_=grp[:, h].rearrange("p u m t -> p (u m t)")
+            )
+
+        def scale_w2(h):
+            for j in range(4):
+                nc.vector.tensor_scalar(
+                    out=ws2[:, h, :, 128 * j : 128 * j + 128],
+                    in0=wide2[:, h, :, 128 * j : 128 * j + 128],
+                    scalar1=s[:, 1, h, j : j + 1],
+                    scalar2=None,
+                    op0=ALU.mult,
+                )
+
+        def turn_w2(h):
+            for tt in range(2):
+                bank = psum.tile([P, 2, 2, P], F32, name="w2b", tag="xtb")
+                for t in range(2):
+                    words = ws2[:, h, 2 * tt + t, :].bitcast(F32)
+                    for u in range(2):
+                        nc.tensor.transpose(bank[:, t, u, :], words[:, u::2], ident[:])
+                nc.scalar.copy(
+                    out=grp2[:, h, 2 * tt : 2 * tt + 2, :, :].bitcast(F32), in_=bank[:].rearrange("p t u m -> p t m u")
+                )
+
+        def first_product(b):
+            HB[b] = []
+            for r in range(2):
+                hb = psum.tile([P, 4, P], F32, name="hb")
+                cols = slice(128 * r, 128 * r + 128)
+                for u in range(4):
+                    for h in range(2):
+                        wc = slice(128 * u, 128 * u + 128)
+                        nc.tensor.matmul_mx(
+                            out=hb[:, u, :],
+                            lhsT=w1c[:, h, wc].bitcast(X4),
+                            lhsT_scale=w1s[:, h, wc],
+                            rhs=XC[b][:, h, cols].bitcast(X4),
+                            rhs_scale=XS[b][:, h, cols],
+                            start=(h == 0),
+                            stop=(h == 1),
+                        )
+                HB[b].append(hb)
+
+        def weigh(b):
+            HG[b] = work.tile([P, 2, P, 4], BF16, name="hg", align_bytes=64)
+            for r in range(2):
+                nc.vector.tensor_tensor(
+                    out=HG[b][:, r, :, :],
+                    in0=HB[b][r][:].rearrange("p u n -> p n u"),
+                    in1=a4[:].unsqueeze(1).to_broadcast([P, P, 4]),
+                    op=ALU.mult,
+                )
+
+        def quantize_h(b):
+            HC[b] = work.tile([P, 256], U32, name="hc", align_bytes=64)
+            HS[b] = work.tile([P, 256], U8, name="hs", align_bytes=64)
+            nc.vector.quantize_mx(out=HC[b][:].bitcast(X4), scales=HS[b][:], in_=HG[b][:].rearrange("p r n t -> p (r n t)"))
+
+        def second_product(b, part):
+            tag = "ya" if part == 0 else "yb"
+            Y[b, part] = []
+            for i in range(2):
+                yb = psum.tile([P, 512], F32, name="y", tag=tag)
+                if KIND[b] != "D":
+                    for k in range(2):
+                        wc = slice(256 * i + 128 * k, 256 * i + 128 * k + 128)
+                        nc.tensor.matmul_mx(
+                            out=yb[:, 256 * k : 256 * k + 256],
+                            lhsT=w2c[:, part, wc].bitcast(X4),
+                            lhsT_scale=w2s[:, part, wc],
+                            rhs=HC[b][:].bitcast(X4),
+                            rhs_scale=HS[b][:],
+                            start=True,
+                            stop=True,
+                        )
+                else:
+                    cols = slice(128 * part, 128 * part + 128)
+                    nc.tensor.matmul_mx(
+                        out=yb[:],
+                        lhsT=HC[b][:, cols].bitcast(X4),
+                        lhsT_scale=HS[b][:, cols],
+                        rhs=w2c[:, i, :].bitcast(X4),
+                        rhs_scale=w2s[:, i, :],
+                        start=True,
+                        stop=True,
+                    )
+                Y[b, part].append(yb)
+
+        def standardise(b, r, eng):
+            if KIND[b] != "D" or XG[b][r] != eng:
+                return
+            xg = work.tile([P, D], F32, name="xg", align_bytes=64, bufs=5)
+            e = nc.gpsimd if eng == "G" else nc.vector
+            e.tensor_tensor(out=xg[:], in0=X[b][:, r, :], in1=gb[:], op=ALU.mult)
+            XGT[b, r] = xg
+
+        def subtract(b, part):
+            if part == 0:
+                O[b] = work.tile([P, 2, D], F32, name="o", align_bytes=64)
+            if KIND[b] == "T":
+                et = work.tile([P, 4, 256], F32, name="et", align_bytes=64, bufs=4)
+                for t in range(4):
+                    nc.vector.scalar_tensor_tensor(
+                        out=et[:, t, :],
+                        in0=GX[b][:, part, :, t],
+                        scalar=gt[:, part, t : t + 1],
+                        in1=Y[b, part][t // 2][:, 256 * (t % 2) : 256 * (t % 2) + 256],
+                        op0=ALU.mult,
+                        op1=ALU.subtract,
+                    )
+                ET[b, part] = et
+            elif KIND[b] == "U":
+                et = work.tile([P, 4, 256], F32, name="et", align_bytes=64, bufs=4)
+                for i in range(2):
+                    nc.scalar.activation(
+                        out=et[:, 2 * i : 2 * i + 2, :].rearrange("p t n -> p (t n)"),
+                        in_=Y[b, part][i][:],
+                        func=ACT.Copy,
+                        scale=-1.0,
+                    )
+                ET[b, part] = et
+            else:
+                for h in range(2):
+                    c = slice(512 * h, 512 * h + 512)
+                    nc.vector.tensor_tensor(
+                        out=O[b][:, part, c].rearrange("p (m t) -> p m t", t=4),
+                        in0=XGT[b, part][:, c].rearrange("p (m t) -> p m t", t=4),
+                        in1=Y[b, part][h][:].rearrange("p (t m) -> p m t", t=4),
+                        op=ALU.subtract,
+                    )
+
+        def turn_back(b, part):
+            tag = "ya" if part == 0 else "yb"
+            et = ET[b, part]
+            for r in range(2):
+                ob = psum.tile([P, 4, P], F32, name="ob", tag=tag)
+                cols = slice(128 * r, 128 * r + 128)
+                for t in range(4):
+                    nc.tensor.transpose(ob[:, t, :], et[:, t, cols], ident[:])
+                nc.scalar.activation(
+                    out=O[b][:, r, 512 * part : 512 * part + 512].rearrange("p (m t) -> p m t", t=4),
+                    in_=ob[:].rearrange("p t m -> p m t"),
+                    func=ACT.Square,
+                )
+
+        def finish(b):
+            if KIND[b] != "D":
+                nc.sync.dma_start(out=ov[b], in_=O[b][:])
+                return
+            for r in range(2):
+                nc.scalar.activation(out=O[b][:, r, :], in_=O[b][:, r, :], func=ACT.Square)
+                nc.sync.dma_start(out=ov[b][:, r, :], in_=O[b][:, r, :])
+
+        def ok(b):
+            return 0 <= b < NP
+
+        transposes(0)
+        widen("V", wide1, b1, 0)
+        widen("S", wide1, b1, 1)
+        for j in range(4):
+            group_w1("V", 0, j)
+        quantize_w(w1c, w1s, grp1, 0)
+        for j in range(2):
+            group_w1("V", 1, j)
+        for j in range(2):
+            group_w1("S", 1, 2 + j)
+        transposes(1)
+        quantize_x(0)
+        quantize_w(w1c, w1s, grp1, 1)
+        first_product(0)
+        widen("V", wide2, b2, 0)
+        widen("S", wide2, b2, 1)
+        transposes(2)
+        quantize_x(1)
+        for r in range(2):
+            standardise(0, r, "G")
+            standardise(0, r, "V")
+        scale_w2(0)
+        weigh(0)
+        turn_w2(0)
+        scale_w2(1)
+        quantize_h(0)
+        turn_w2(1)
+        first_product(1)
+        transposes(3)
+        quantize_w(w2c, w2s, grp2, 0)
+        quantize_x(2)
+        quantize_w(w2c, w2s, grp2, 1)
+        second_product(0, 0)
+        second_product(0, 1)
+        for r in range(2):
+            standardise(1, r, "G")
+            standardise(1, r, "V")
+
+        for p in range(NP):
+            if ok(p + 8):
+                load_x(p + 8)
+            if KIND[p] == "U":
+                subtract(p, 0)
+                subtract(p, 1)
+            if ok(p + 1):
+                weigh(p + 1)
+            if ok(p + 2):
+                first_product(p + 2)
+            if ok(p + 4):
+                transposes(p + 4)
+            if KIND[p] == "U":
+                turn_back(p, 0)
+                turn_back(p, 1)
+            for part in range(2):
+                if KIND[p] == "D":
+                    subtract(p, part)
+                elif KIND[p] == "T":
+                    subtract(p, part)
+                    turn_back(p, part)
+            if ok(p + 1):
+                quantize_h(p + 1)
+                second_product(p + 1, 0)
+                second_product(p + 1, 1)
+            if ok(p + 3):
+                quantize_x(p + 3)
+            if ok(p + 2):
+                for r in range(2):
+                    standardise(p + 2, r, "G")
+                    standardise(p + 2, r, "V")
+            finish(p)

@@ -17,8 +17,7 @@ ACT = mybir.ActivationFunctionType
 
 P = 128
 NP = T // 256
-KIND = "DDTDDTDDTDDTDTDD"
-XG = ["GG","GG","GG","GG","GG","GG","GG","GG","GG","GG","GG","GG","GG","GG","GG","GG"]
+KIND = "TDTDTDTDTDTDTDTD"
 
 
 def tile_sensor_residual_squared_d7_kernel(tc, x, g, a, w1_bytes, w1_scale, w2_bytes, w2_scale, out):
@@ -39,27 +38,29 @@ def tile_sensor_residual_squared_d7_kernel(tc, x, g, a, w1_bytes, w1_scale, w2_b
             nc.sync.dma_start(out=xt[:].rearrange("p r d -> p (r d)"), in_=xv[b])
             X[b] = xt
 
+        sall = keep.tile([P, 2, 32], F32, name="sall")
+        nc.scalar.dma_start(out=sall[:, 0, :], in_=w1_scale.rearrange("i j -> (i j)").partition_broadcast(P))
         b1 = keep.tile([P, 2, 2048], U8, name="b1", align_bytes=64)
         b2 = keep.tile([P, 2, 2048], U8, name="b2", align_bytes=64)
         w1v = w1_bytes.rearrange("(g p t) n -> p g (t n)", p=P, t=4)
         w2v = w2_bytes.rearrange("(g p t) n -> p g (t n)", p=P, t=4)
-        nc.sync.dma_start(out=b1[:, 0, :], in_=w1v[:, 0, :])
-        load_x(0)
-        nc.sync.dma_start(out=b1[:, 1, :], in_=w1v[:, 1, :])
-        sall = keep.tile([P, 2, 32], F32, name="sall")
-        nc.scalar.dma_start(out=sall[:, 0, :], in_=w1_scale.rearrange("i j -> (i j)").partition_broadcast(P))
+        for h in range(2):
+            nc.sync.dma_start(out=b1[:, h, :], in_=w1v[:, h, :])
         nc.scalar.dma_start(out=sall[:, 1, :], in_=w2_scale.rearrange("i j -> (i j)").partition_broadcast(P))
         a4 = keep.tile([P, 4], BF16, name="a4")
         nc.scalar.dma_start(out=a4[:], in_=a.rearrange("(p t) -> p t", t=4))
-        for h in range(2):
-            nc.sync.dma_start(out=b2[:, h, :], in_=w2v[:, h, :])
-        load_x(1)
-        gb = keep.tile([P, D], BF16, name="gb", align_bytes=64)
-        nc.scalar.dma_start(out=gb[:], in_=g.partition_broadcast(P))
         gt = keep.tile([P, 2, 4], BF16, name="gt")
         nc.scalar.dma_start(out=gt[:], in_=g.rearrange("(g p t) -> p g t", p=P, t=4))
-        for b in range(2, 8):
+        load_x(0)
+        for h in range(2):
+            nc.sync.dma_start(out=b2[:, h, :], in_=w2v[:, h, :])
+        for b in range(1, 4):
             load_x(b)
+        for b in range(4, 8):
+            load_x(b)
+        graw = keep.tile([P, D], BF16, name="graw", align_bytes=64)
+        nc.sync.dma_start(out=graw[:], in_=g.partition_broadcast(P))
+        gb = keep.tile([P, D], BF16, name="gb", align_bytes=64)
 
         ident = keep.tile([P, P], F32, name="ident", align_bytes=64)
         make_identity(nc, ident[:])
@@ -73,7 +74,7 @@ def tile_sensor_residual_squared_d7_kernel(tc, x, g, a, w1_bytes, w1_scale, w2_b
             )
 
         def transposes(b):
-            GX[b] = work.tile([P, 2, 256, 4], BF16, name="gx", align_bytes=64, bufs=7)
+            GX[b] = work.tile([P, 2, 256, 4], BF16, name="gx", align_bytes=64, bufs=8)
             for r in range(2):
                 bank = psum.tile([P, 2, 2, P], F32, name="xtb")
                 words = X[b][:, r, :].bitcast(F32)
@@ -98,7 +99,6 @@ def tile_sensor_residual_squared_d7_kernel(tc, x, g, a, w1_bytes, w1_scale, w2_b
         w2c = keep.tile([P, 2, 512], U32, name="w2c", align_bytes=64)
         w2s = keep.tile([P, 2, 512], U8, name="w2s", align_bytes=64)
         wide1 = keep.tile([P, 2, 4, 512], BF16, name="wide1", align_bytes=64)
-        wide2 = keep.tile([P, 2, 4, 512], BF16, name="wide2", align_bytes=64)
         grp1 = keep.tile([P, 2, 4, P, 4], BF16, name="grp1", align_bytes=64)
         ws2 = keep.tile([P, 2, 4, 512], BF16, name="ws2", align_bytes=64)
         grp2 = keep.tile([P, 2, 4, P, 4], BF16, name="grp2", align_bytes=64)
@@ -127,14 +127,16 @@ def tile_sensor_residual_squared_d7_kernel(tc, x, g, a, w1_bytes, w1_scale, w2_b
             )
 
         def scale_w2(h):
-            for j in range(4):
-                nc.vector.tensor_scalar(
-                    out=ws2[:, h, :, 128 * j : 128 * j + 128],
-                    in0=wide2[:, h, :, 128 * j : 128 * j + 128],
-                    scalar1=s[:, 1, h, j : j + 1],
-                    scalar2=None,
-                    op0=ALU.mult,
-                )
+            for t in range(4):
+                for j in range(4):
+                    c = 512 * t + 128 * j
+                    nc.vector.tensor_scalar(
+                        out=ws2[:, h, t, 128 * j : 128 * j + 128],
+                        in0=b2[:, h, c : c + 128].bitcast(E4M3),
+                        scalar1=s[:, 1, h, j : j + 1],
+                        scalar2=None,
+                        op0=ALU.mult,
+                    )
 
         def turn_w2(h):
             for tt in range(2):
@@ -177,12 +179,12 @@ def tile_sensor_residual_squared_d7_kernel(tc, x, g, a, w1_bytes, w1_scale, w2_b
                 )
 
         def quantize_h(b):
-            HC[b] = work.tile([P, 256], U32, name="hc", align_bytes=64)
-            HS[b] = work.tile([P, 256], U8, name="hs", align_bytes=64)
+            HC[b] = work.tile([P, 256], U32, name="hc", align_bytes=64, bufs=4)
+            HS[b] = work.tile([P, 256], U8, name="hs", align_bytes=64, bufs=4)
             nc.vector.quantize_mx(out=HC[b][:].bitcast(X4), scales=HS[b][:], in_=HG[b][:].rearrange("p r n t -> p (r n t)"))
 
         def second_product(b, part):
-            tag = "ya" if part == 0 else "yb"
+            tag = "ya" if KIND[b] == "D" else "yb"
             Y[b, part] = []
             for i in range(2):
                 yb = psum.tile([P, 512], F32, name="y", tag=tag)
@@ -212,16 +214,14 @@ def tile_sensor_residual_squared_d7_kernel(tc, x, g, a, w1_bytes, w1_scale, w2_b
                 Y[b, part].append(yb)
 
         def standardise(b, r, eng):
-            if KIND[b] != "D" or XG[b][r] != eng:
-                return
-            xg = work.tile([P, D], F32, name="xg", align_bytes=64, bufs=5)
+            xg = work.tile([P, D], F32, name="xg", align_bytes=64, bufs=2)
             e = nc.gpsimd if eng == "G" else nc.vector
-            e.tensor_tensor(out=xg[:], in0=X[b][:, r, :], in1=gb[:], op=ALU.mult)
+            e.tensor_tensor(out=xg[:], in0=X[b][:, r, :], in1=(gb if eng == "G" else graw)[:], op=ALU.mult)
             XGT[b, r] = xg
 
-        def subtract(b, part):
-            if part == 0:
-                O[b] = work.tile([P, 2, D], F32, name="o", align_bytes=64)
+        def subtract(b, part, halves=(0, 1)):
+            if b not in O:
+                O[b] = work.tile([P, 2, D], F32, name="o", align_bytes=64, bufs=4)
             if KIND[b] == "T":
                 et = work.tile([P, 4, 256], F32, name="et", align_bytes=64, bufs=4)
                 for t in range(4):
@@ -245,7 +245,7 @@ def tile_sensor_residual_squared_d7_kernel(tc, x, g, a, w1_bytes, w1_scale, w2_b
                     )
                 ET[b, part] = et
             else:
-                for h in range(2):
+                for h in halves:
                     c = slice(512 * h, 512 * h + 512)
                     nc.vector.tensor_tensor(
                         out=O[b][:, part, c].rearrange("p (m t) -> p m t", t=4),
@@ -255,7 +255,7 @@ def tile_sensor_residual_squared_d7_kernel(tc, x, g, a, w1_bytes, w1_scale, w2_b
                     )
 
         def turn_back(b, part):
-            tag = "ya" if part == 0 else "yb"
+            tag = "yb"
             et = ET[b, part]
             for r in range(2):
                 ob = psum.tile([P, 4, P], F32, name="ob", tag=tag)
@@ -268,84 +268,86 @@ def tile_sensor_residual_squared_d7_kernel(tc, x, g, a, w1_bytes, w1_scale, w2_b
                     func=ACT.Square,
                 )
 
-        def finish(b):
-            if KIND[b] != "D":
-                nc.sync.dma_start(out=ov[b], in_=O[b][:])
+        def finish(b, r):
+            if (b, r) == (NP - 1, 1):
+                nc.scalar.activation(out=O[b][:, r, 0:512], in_=O[b][:, r, 0:512], func=ACT.Square)
+                nc.sync.dma_start(out=ov[b][:, r, 0:512], in_=O[b][:, r, 0:512])
+                nc.vector.tensor_tensor(out=O[b][:, r, 512:], in0=O[b][:, r, 512:], in1=O[b][:, r, 512:], op=ALU.mult)
+                nc.sync.dma_start(out=ov[b][:, r, 512:], in_=O[b][:, r, 512:])
                 return
-            for r in range(2):
-                nc.scalar.activation(out=O[b][:, r, :], in_=O[b][:, r, :], func=ACT.Square)
-                nc.sync.dma_start(out=ov[b][:, r, :], in_=O[b][:, r, :])
+            nc.scalar.activation(out=O[b][:, r, :], in_=O[b][:, r, :], func=ACT.Square)
+            nc.sync.dma_start(out=ov[b][:, r, :], in_=O[b][:, r, :])
 
         def ok(b):
             return 0 <= b < NP
 
-        transposes(0)
+
+        def tile_of(k):
+            return (2 * (k // 2) + 1, k % 2) if 0 <= k < NP else None
+
+        def part_of(k):
+            return (2 * (k // 2), k % 2) if 0 <= k < NP else None
+
         widen("V", wide1, b1, 0)
         widen("S", wide1, b1, 1)
         for j in range(4):
             group_w1("V", 0, j)
-        quantize_w(w1c, w1s, grp1, 0)
-        for j in range(2):
-            group_w1("V", 1, j)
         for j in range(2):
             group_w1("S", 1, 2 + j)
+        for j in range(2):
+            group_w1("V", 1, j)
+        quantize_w(w1c, w1s, grp1, 0)
+        quantize_w(w1c, w1s, grp1, 1)
+        transposes(0)
         transposes(1)
         quantize_x(0)
-        quantize_w(w1c, w1s, grp1, 1)
         first_product(0)
-        widen("V", wide2, b2, 0)
-        widen("S", wide2, b2, 1)
-        transposes(2)
-        quantize_x(1)
-        for r in range(2):
-            standardise(0, r, "G")
-            standardise(0, r, "V")
         scale_w2(0)
-        weigh(0)
         turn_w2(0)
+        weigh(0)
+        transposes(2)
         scale_w2(1)
-        quantize_h(0)
-        turn_w2(1)
+        quantize_x(1)
         first_product(1)
-        transposes(3)
+        turn_w2(1)
         quantize_w(w2c, w2s, grp2, 0)
+        quantize_h(0)
         quantize_x(2)
+        weigh(1)
+        first_product(2)
         quantize_w(w2c, w2s, grp2, 1)
-        second_product(0, 0)
-        second_product(0, 1)
-        for r in range(2):
-            standardise(1, r, "G")
-            standardise(1, r, "V")
-
-        for p in range(NP):
-            if ok(p + 8):
-                load_x(p + 8)
-            if KIND[p] == "U":
-                subtract(p, 0)
-                subtract(p, 1)
-            if ok(p + 1):
-                weigh(p + 1)
-            if ok(p + 2):
-                first_product(p + 2)
-            if ok(p + 4):
-                transposes(p + 4)
-            if KIND[p] == "U":
-                turn_back(p, 0)
-                turn_back(p, 1)
-            for part in range(2):
-                if KIND[p] == "D":
-                    subtract(p, part)
-                elif KIND[p] == "T":
-                    subtract(p, part)
-                    turn_back(p, part)
-            if ok(p + 1):
-                quantize_h(p + 1)
-                second_product(p + 1, 0)
-                second_product(p + 1, 1)
-            if ok(p + 3):
-                quantize_x(p + 3)
-            if ok(p + 2):
-                for r in range(2):
-                    standardise(p + 2, r, "G")
-                    standardise(p + 2, r, "V")
-            finish(p)
+        transposes(3)
+        for b in range(NP + 2):
+            if ok(b + 8):
+                load_x(b + 8)
+            dt, pt, nt, old = tile_of(b - 1), part_of(b), tile_of(b), part_of(b - 1)
+            if dt:
+                subtract(*dt, halves=(0,))
+            if ok(b + 1):
+                quantize_h(b + 1)
+            if dt:
+                subtract(*dt, halves=(1,))
+            if ok(b + 3):
+                quantize_x(b + 3)
+            if old:
+                turn_back(*old)
+                nc.sync.dma_start(
+                    out=ov[old[0]][:, :, 512 * old[1] : 512 * old[1] + 512], in_=O[old[0]][:, :, 512 * old[1] : 512 * old[1] + 512]
+                )
+            if ok(b + 4):
+                transposes(b + 4)
+            if b == 0:
+                nc.scalar.copy(out=gb[:], in_=graw[:])
+            if pt:
+                second_product(*pt)
+            if ok(b + 2):
+                weigh(b + 2)
+            if nt:
+                second_product(*nt)
+                standardise(*nt, "V" if b == 0 else "G")
+            if ok(b + 3):
+                first_product(b + 3)
+            if pt:
+                subtract(*pt)
+            if dt:
+                finish(*dt)

@@ -17,6 +17,10 @@ ACT = mybir.ActivationFunctionType
 
 P = 128
 NP = T // 256
+UFROM = 99
+DGSTEP = -1
+XGV = [0]
+SW = []
 KIND = "TDTDTDTDTDTDTDTD"
 
 
@@ -73,17 +77,17 @@ def tile_sensor_residual_squared_d7_kernel(tc, x, g, a, w1_bytes, w1_scale, w2_b
                 in_=sall[rows].rearrange("p w (h q j) -> p w h q j", q=4, j=4)[:, :, :, q, :],
             )
 
-        def transposes(b):
-            GX[b] = work.tile([P, 2, 256, 4], BF16, name="gx", align_bytes=64, bufs=8)
-            for r in range(2):
-                bank = psum.tile([P, 2, 2, P], F32, name="xtb")
-                words = X[b][:, r, :].bitcast(F32)
-                for h in range(2):
-                    for u in range(2):
-                        nc.tensor.transpose(bank[:, h, u, :], words[:, 256 * h + u : 256 * (h + 1) : 2], ident[:])
-                nc.scalar.copy(
-                    out=GX[b][:, :, 128 * r : 128 * r + 128, :].bitcast(F32), in_=bank[:].rearrange("p h u n -> p h n u")
-                )
+        def turn_x(b, r):
+            if r == 0:
+                GX[b] = work.tile([P, 2, 256, 4], BF16, name="gx", align_bytes=64, bufs=8)
+            bank = psum.tile([P, 2, 2, P], F32, name="xtb")
+            words = X[b][:, r, :].bitcast(F32)
+            for h in range(2):
+                for u in range(2):
+                    nc.tensor.transpose(bank[:, h, u, :], words[:, 256 * h + u : 256 * (h + 1) : 2], ident[:])
+            nc.scalar.copy(
+                out=GX[b][:, :, 128 * r : 128 * r + 128, :].bitcast(F32), in_=bank[:].rearrange("p h u n -> p h n u")
+            )
 
         def quantize_x(b):
             XC[b] = work.tile([P, 2, 256], U32, name="xc", align_bytes=64)
@@ -99,6 +103,7 @@ def tile_sensor_residual_squared_d7_kernel(tc, x, g, a, w1_bytes, w1_scale, w2_b
         w2c = keep.tile([P, 2, 512], U32, name="w2c", align_bytes=64)
         w2s = keep.tile([P, 2, 512], U8, name="w2s", align_bytes=64)
         wide1 = keep.tile([P, 2, 4, 512], BF16, name="wide1", align_bytes=64)
+        wide2 = keep.tile([P, 2, 4, 512], BF16, name="wide2", align_bytes=64)
         grp1 = keep.tile([P, 2, 4, P, 4], BF16, name="grp1", align_bytes=64)
         ws2 = keep.tile([P, 2, 4, 512], BF16, name="ws2", align_bytes=64)
         grp2 = keep.tile([P, 2, 4, P, 4], BF16, name="grp2", align_bytes=64)
@@ -126,17 +131,34 @@ def tile_sensor_residual_squared_d7_kernel(tc, x, g, a, w1_bytes, w1_scale, w2_b
                 out=codes[:, h, :].bitcast(X4), scales=scales[:, h, :], in_=grp[:, h].rearrange("p u m t -> p (u m t)")
             )
 
-        def scale_w2(h):
+        dg = keep.tile([P, 8, P], BF16, name="dg", align_bytes=64)
+        gt32 = keep.tile([P, 8], F32, name="gt32")
+
+        def make_dg():
+            nc.scalar.copy(out=gt32[:], in_=gt[:].rearrange("p h t -> p (h t)"))
+            for i in range(8):
+                nc.scalar.activation(out=dg[:, i, :], in_=ident[:], func=ACT.Copy, scale=gt32[:, i : i + 1])
+
+        def scale_w2_s(h):
             for t in range(4):
                 for j in range(4):
                     c = 512 * t + 128 * j
-                    nc.vector.tensor_scalar(
+                    nc.scalar.activation(
                         out=ws2[:, h, t, 128 * j : 128 * j + 128],
-                        in0=b2[:, h, c : c + 128].bitcast(E4M3),
-                        scalar1=s[:, 1, h, j : j + 1],
-                        scalar2=None,
-                        op0=ALU.mult,
+                        in_=b2[:, h, c : c + 128].bitcast(E4M3),
+                        func=ACT.Copy,
+                        scale=s[:, 1, h, j : j + 1],
                     )
+
+        def scale_w2(h):
+            for j in range(4):
+                nc.vector.tensor_scalar(
+                    out=ws2[:, h, :, 128 * j : 128 * j + 128],
+                    in0=wide2[:, h, :, 128 * j : 128 * j + 128],
+                    scalar1=s[:, 1, h, j : j + 1],
+                    scalar2=None,
+                    op0=ALU.mult,
+                )
 
         def turn_w2(h):
             for tt in range(2):
@@ -149,34 +171,32 @@ def tile_sensor_residual_squared_d7_kernel(tc, x, g, a, w1_bytes, w1_scale, w2_b
                     out=grp2[:, h, 2 * tt : 2 * tt + 2, :, :].bitcast(F32), in_=bank[:].rearrange("p t u m -> p t m u")
                 )
 
-        def first_product(b):
-            HB[b] = []
-            for r in range(2):
-                hb = psum.tile([P, 4, P], F32, name="hb")
-                cols = slice(128 * r, 128 * r + 128)
-                for u in range(4):
-                    for h in range(2):
-                        wc = slice(128 * u, 128 * u + 128)
-                        nc.tensor.matmul_mx(
-                            out=hb[:, u, :],
-                            lhsT=w1c[:, h, wc].bitcast(X4),
-                            lhsT_scale=w1s[:, h, wc],
-                            rhs=XC[b][:, h, cols].bitcast(X4),
-                            rhs_scale=XS[b][:, h, cols],
-                            start=(h == 0),
-                            stop=(h == 1),
-                        )
-                HB[b].append(hb)
+        def first_product(b, r):
+            hb = psum.tile([P, 4, P], F32, name="hb")
+            cols = slice(128 * r, 128 * r + 128)
+            for u in range(4):
+                for h in range(2):
+                    wc = slice(128 * u, 128 * u + 128)
+                    nc.tensor.matmul_mx(
+                        out=hb[:, u, :],
+                        lhsT=w1c[:, h, wc].bitcast(X4),
+                        lhsT_scale=w1s[:, h, wc],
+                        rhs=XC[b][:, h, cols].bitcast(X4),
+                        rhs_scale=XS[b][:, h, cols],
+                        start=(h == 0),
+                        stop=(h == 1),
+                    )
+            HB[b, r] = hb
 
-        def weigh(b):
-            HG[b] = work.tile([P, 2, P, 4], BF16, name="hg", align_bytes=64)
-            for r in range(2):
-                nc.vector.tensor_tensor(
-                    out=HG[b][:, r, :, :],
-                    in0=HB[b][r][:].rearrange("p u n -> p n u"),
-                    in1=a4[:].unsqueeze(1).to_broadcast([P, P, 4]),
-                    op=ALU.mult,
-                )
+        def weigh(b, r):
+            if r == 0:
+                HG[b] = work.tile([P, 2, P, 4], BF16, name="hg", align_bytes=64)
+            nc.vector.tensor_tensor(
+                out=HG[b][:, r, :, :],
+                in0=HB[b, r][:].rearrange("p u n -> p n u"),
+                in1=a4[:].unsqueeze(1).to_broadcast([P, P, 4]),
+                op=ALU.mult,
+            )
 
         def quantize_h(b):
             HC[b] = work.tile([P, 256], U32, name="hc", align_bytes=64, bufs=4)
@@ -219,12 +239,24 @@ def tile_sensor_residual_squared_d7_kernel(tc, x, g, a, w1_bytes, w1_scale, w2_b
             e.tensor_tensor(out=xg[:], in0=X[b][:, r, :], in1=(gb if eng == "G" else graw)[:], op=ALU.mult)
             XGT[b, r] = xg
 
-        def subtract(b, part, halves=(0, 1)):
+        def subtract(b, part, halves):
             if b not in O:
                 O[b] = work.tile([P, 2, D], F32, name="o", align_bytes=64, bufs=4)
-            if KIND[b] == "T":
-                et = work.tile([P, 4, 256], F32, name="et", align_bytes=64, bufs=4)
-                for t in range(4):
+            if KIND[b] == "T" and b + part >= UFROM:
+                if 0 in halves:
+                    ET[b, part] = work.tile([P, 4, 256], F32, name="et", align_bytes=64, bufs=4)
+                for i in halves:
+                    nc.scalar.activation(
+                        out=ET[b, part][:, 2 * i : 2 * i + 2, :].rearrange("p t n -> p (t n)"),
+                        in_=Y[b, part][i][:],
+                        func=ACT.Copy,
+                        scale=-1.0,
+                    )
+            elif KIND[b] == "T":
+                if 0 in halves:
+                    ET[b, part] = work.tile([P, 4, 256], F32, name="et", align_bytes=64, bufs=4)
+                et = ET[b, part]
+                for t in [2 * i + k for i in halves for k in range(2)]:
                     nc.vector.scalar_tensor_tensor(
                         out=et[:, t, :],
                         in0=GX[b][:, part, :, t],
@@ -233,17 +265,6 @@ def tile_sensor_residual_squared_d7_kernel(tc, x, g, a, w1_bytes, w1_scale, w2_b
                         op0=ALU.mult,
                         op1=ALU.subtract,
                     )
-                ET[b, part] = et
-            elif KIND[b] == "U":
-                et = work.tile([P, 4, 256], F32, name="et", align_bytes=64, bufs=4)
-                for i in range(2):
-                    nc.scalar.activation(
-                        out=et[:, 2 * i : 2 * i + 2, :].rearrange("p t n -> p (t n)"),
-                        in_=Y[b, part][i][:],
-                        func=ACT.Copy,
-                        scale=-1.0,
-                    )
-                ET[b, part] = et
             else:
                 for h in halves:
                     c = slice(512 * h, 512 * h + 512)
@@ -254,19 +275,36 @@ def tile_sensor_residual_squared_d7_kernel(tc, x, g, a, w1_bytes, w1_scale, w2_b
                         op=ALU.subtract,
                     )
 
-        def turn_back(b, part):
-            tag = "yb"
+        def turn_back(b, part, r):
             et = ET[b, part]
-            for r in range(2):
-                ob = psum.tile([P, 4, P], F32, name="ob", tag=tag)
-                cols = slice(128 * r, 128 * r + 128)
-                for t in range(4):
-                    nc.tensor.transpose(ob[:, t, :], et[:, t, cols], ident[:])
-                nc.scalar.activation(
-                    out=O[b][:, r, 512 * part : 512 * part + 512].rearrange("p (m t) -> p m t", t=4),
-                    in_=ob[:].rearrange("p t m -> p m t"),
-                    func=ACT.Square,
-                )
+            ob = psum.tile([P, 4, P], F32, name="ob", tag="yb")
+            for t in range(4):
+                if b + part >= UFROM:
+                    nc.tensor.matmul(
+                        ob[:, t, :],
+                        lhsT=GX[b][:, part, 128 * r : 128 * r + 128, t],
+                        rhs=dg[:, 4 * part + t, :],
+                        start=True,
+                        stop=False,
+                    )
+                    nc.tensor.matmul(
+                        ob[:, t, :],
+                        lhsT=et[:, t, 128 * r : 128 * r + 128],
+                        rhs=ident[:],
+                        is_transpose=True,
+                        start=False,
+                        stop=True,
+                    )
+                else:
+                    nc.tensor.transpose(ob[:, t, :], et[:, t, 128 * r : 128 * r + 128], ident[:])
+            c = slice(512 * part, 512 * part + 512)
+            nc.scalar.activation(
+                out=O[b][:, r, c].rearrange("p (m t) -> p m t", t=4),
+                in_=ob[:].rearrange("p t m -> p m t"),
+                func=ACT.Square,
+            )
+            if r == 1:
+                nc.sync.dma_start(out=ov[b][:, :, c], in_=O[b][:, :, c])
 
         def finish(b, r):
             if (b, r) == (NP - 1, 1):
@@ -288,66 +326,85 @@ def tile_sensor_residual_squared_d7_kernel(tc, x, g, a, w1_bytes, w1_scale, w2_b
         def part_of(k):
             return (2 * (k // 2), k % 2) if 0 <= k < NP else None
 
-        widen("V", wide1, b1, 0)
         widen("S", wide1, b1, 1)
-        for j in range(4):
-            group_w1("V", 0, j)
-        for j in range(2):
-            group_w1("S", 1, 2 + j)
+        for j in range(2, 4):
+            group_w1("S", 1, j)
+        widen("V", wide1, b1, 0)
         for j in range(2):
             group_w1("V", 1, j)
-        quantize_w(w1c, w1s, grp1, 0)
+        turn_x(0, 0)
+        turn_x(0, 1)
+        widen("S", wide2, b2, 0)
+        for j in range(4):
+            group_w1("V", 0, j)
+        turn_x(1, 0)
         quantize_w(w1c, w1s, grp1, 1)
-        transposes(0)
-        transposes(1)
+        quantize_w(w1c, w1s, grp1, 0)
         quantize_x(0)
-        first_product(0)
+        turn_x(1, 1)
         scale_w2(0)
-        turn_w2(0)
-        weigh(0)
-        transposes(2)
-        scale_w2(1)
+        widen("S", wide2, b2, 1)
         quantize_x(1)
-        first_product(1)
-        turn_w2(1)
-        quantize_w(w2c, w2s, grp2, 0)
-        quantize_h(0)
+        scale_w2(1)
+        first_product(0, 0)
+        turn_x(2, 0)
+        turn_x(2, 1)
+        first_product(0, 1)
+        turn_w2(0)
+        weigh(0, 0)
+        weigh(0, 1)
         quantize_x(2)
-        weigh(1)
-        first_product(2)
+        first_product(1, 0)
+        weigh(1, 0)
+        turn_w2(1)
+        first_product(1, 1)
+        turn_x(3, 0)
+        weigh(1, 1)
+        quantize_h(0)
+        turn_x(3, 1)
         quantize_w(w2c, w2s, grp2, 1)
-        transposes(3)
+        first_product(2, 0)
+        quantize_w(w2c, w2s, grp2, 0)
+        first_product(2, 1)
         for b in range(NP + 2):
-            if ok(b + 8):
-                load_x(b + 8)
             dt, pt, nt, old = tile_of(b - 1), part_of(b), tile_of(b), part_of(b - 1)
             if dt:
-                subtract(*dt, halves=(0,))
+                subtract(*dt, (0,))
+            if old:
+                turn_back(*old, 0)
             if ok(b + 1):
                 quantize_h(b + 1)
-            if dt:
-                subtract(*dt, halves=(1,))
             if ok(b + 3):
                 quantize_x(b + 3)
+            if ok(b + 8):
+                load_x(b + 8)
             if old:
-                turn_back(*old)
-                nc.sync.dma_start(
-                    out=ov[old[0]][:, :, 512 * old[1] : 512 * old[1] + 512], in_=O[old[0]][:, :, 512 * old[1] : 512 * old[1] + 512]
-                )
+                turn_back(*old, 1)
             if ok(b + 4):
-                transposes(b + 4)
+                turn_x(b + 4, 0)
             if b == 0:
                 nc.scalar.copy(out=gb[:], in_=graw[:])
+            if ok(b + 4):
+                turn_x(b + 4, 1)
             if pt:
                 second_product(*pt)
-            if ok(b + 2):
-                weigh(b + 2)
+            if dt:
+                subtract(*dt, (1,))
             if nt:
                 second_product(*nt)
-                standardise(*nt, "V" if b == 0 else "G")
-            if ok(b + 3):
-                first_product(b + 3)
-            if pt:
-                subtract(*pt)
+            if nt:
+                standardise(*nt, "V" if b in XGV else "G")
+            if ok(b + 2):
+                weigh(b + 2, 0)
             if dt:
                 finish(*dt)
+            if ok(b + 3):
+                first_product(b + 3, 0)
+            if ok(b + 2):
+                weigh(b + 2, 1)
+            if ok(b + 3):
+                first_product(b + 3, 1)
+            if pt:
+                subtract(*pt, (0,))
+            if pt:
+                subtract(*pt, (1,))

@@ -16,395 +16,352 @@ ALU = mybir.AluOpType
 ACT = mybir.ActivationFunctionType
 
 P = 128
-NP = T // 256
-UFROM = 99
-DGSTEP = -1
-XGV = [0]
-SW = []
-KIND = "TDTDTDTDTDTDTDTD"
+PAIRS = T // 256
+AHEAD = 8
 
 
 def tile_sensor_residual_squared_d7_kernel(tc, x, g, a, w1_bytes, w1_scale, w2_bytes, w2_scale, out):
     nc = tc.nc
-    xv = x.rearrange("(b p r) d -> b p (r d)", p=P, r=2)
-    ov = out.rearrange("(b p r) d -> b p r d", p=P, r=2)
+    x_pairs = x.rearrange("(b p r) d -> b p (r d)", p=P, r=2)
+    out_pairs = out.rearrange("(b p r) d -> b p r d", p=P, r=2)
+
     with ExitStack() as ctx:
         keep = ctx.enter_context(tc.tile_pool(name="keep", bufs=1))
-        px = ctx.enter_context(tc.tile_pool(name="px", bufs=10))
+        x_pool = ctx.enter_context(tc.tile_pool(name="x_pool", bufs=AHEAD + 2))
         work = ctx.enter_context(tc.tile_pool(name="work", bufs=3))
         psum = ctx.enter_context(tc.psum_pool(name="psum", bufs=2))
         ctx.enter_context(tc.manual_schedule())
 
-        X, GX, XC, XS, HB, HG, HC, HS, Y, XGT, O, ET = {}, {}, {}, {}, {}, {}, {}, {}, {}, {}, {}, {}
+        x_raw, x_laced, x_codes, x_scales = {}, {}, {}, {}
+        h_sums, h_laced, h_codes, h_scales = {}, {}, {}, {}
+        y_sums, xg, turned, result = {}, {}, {}, {}
 
         def load_x(b):
-            xt = px.tile([P, 2, D], BF16, name="xt", align_bytes=64)
-            nc.sync.dma_start(out=xt[:].rearrange("p r d -> p (r d)"), in_=xv[b])
-            X[b] = xt
+            tile = x_pool.tile([P, 2, D], BF16, name="x_tile", align_bytes=64)
+            nc.sync.dma_start(out=tile[:].rearrange("p r d -> p (r d)"), in_=x_pairs[b])
+            x_raw[b] = tile
 
-        sall = keep.tile([P, 2, 32], F32, name="sall")
-        nc.scalar.dma_start(out=sall[:, 0, :], in_=w1_scale.rearrange("i j -> (i j)").partition_broadcast(P))
-        b1 = keep.tile([P, 2, 2048], U8, name="b1", align_bytes=64)
-        b2 = keep.tile([P, 2, 2048], U8, name="b2", align_bytes=64)
-        w1v = w1_bytes.rearrange("(g p t) n -> p g (t n)", p=P, t=4)
-        w2v = w2_bytes.rearrange("(g p t) n -> p g (t n)", p=P, t=4)
-        for h in range(2):
-            nc.sync.dma_start(out=b1[:, h, :], in_=w1v[:, h, :])
-        nc.scalar.dma_start(out=sall[:, 1, :], in_=w2_scale.rearrange("i j -> (i j)").partition_broadcast(P))
-        a4 = keep.tile([P, 4], BF16, name="a4")
-        nc.scalar.dma_start(out=a4[:], in_=a.rearrange("(p t) -> p t", t=4))
-        gt = keep.tile([P, 2, 4], BF16, name="gt")
-        nc.scalar.dma_start(out=gt[:], in_=g.rearrange("(g p t) -> p g t", p=P, t=4))
+        scales_all = keep.tile([P, 2, 32], F32, name="scales_all")
+        nc.scalar.dma_start(out=scales_all[:, 0, :], in_=w1_scale.rearrange("i j -> (i j)").partition_broadcast(P))
+        w1_raw = keep.tile([P, 2, 4 * R], U8, name="w1_raw", align_bytes=64)
+        w2_raw = keep.tile([P, 2, 4 * R], U8, name="w2_raw", align_bytes=64)
+        w1_rows = w1_bytes.rearrange("(c p t) n -> p c (t n)", p=P, t=4)
+        w2_rows = w2_bytes.rearrange("(c p t) k -> p c (t k)", p=P, t=4)
+        for c in range(2):
+            nc.sync.dma_start(out=w1_raw[:, c, :], in_=w1_rows[:, c, :])
+        nc.scalar.dma_start(out=scales_all[:, 1, :], in_=w2_scale.rearrange("i j -> (i j)").partition_broadcast(P))
+        a_cols = keep.tile([P, 4], BF16, name="a_cols")
+        nc.scalar.dma_start(out=a_cols[:], in_=a.rearrange("(p t) -> p t", t=4))
+        g_cols = keep.tile([P, 2, 4], BF16, name="g_cols")
+        nc.scalar.dma_start(out=g_cols[:], in_=g.rearrange("(c p t) -> p c t", p=P, t=4))
         load_x(0)
-        for h in range(2):
-            nc.sync.dma_start(out=b2[:, h, :], in_=w2v[:, h, :])
-        for b in range(1, 4):
+        for c in range(2):
+            nc.sync.dma_start(out=w2_raw[:, c, :], in_=w2_rows[:, c, :])
+        for b in range(1, AHEAD):
             load_x(b)
-        for b in range(4, 8):
-            load_x(b)
-        graw = keep.tile([P, D], BF16, name="graw", align_bytes=64)
-        nc.sync.dma_start(out=graw[:], in_=g.partition_broadcast(P))
-        gb = keep.tile([P, D], BF16, name="gb", align_bytes=64)
+        g_rows = keep.tile([P, D], BF16, name="g_rows", align_bytes=64)
+        nc.sync.dma_start(out=g_rows[:], in_=g.partition_broadcast(P))
+        g_rows_late = keep.tile([P, D], BF16, name="g_rows_late", align_bytes=64)
 
         ident = keep.tile([P, P], F32, name="ident", align_bytes=64)
         make_identity(nc, ident[:])
 
-        s = keep.tile([P, 2, 2, 4], F32, name="s")
+        scale_cols = keep.tile([P, 2, 2, 4], F32, name="scale_cols")
         for q in range(4):
-            rows = slice(32 * q, 32 * q + 32)
+            quadrant = slice(32 * q, 32 * q + 32)
             nc.vector.tensor_copy(
-                out=s[rows],
-                in_=sall[rows].rearrange("p w (h q j) -> p w h q j", q=4, j=4)[:, :, :, q, :],
+                out=scale_cols[quadrant],
+                in_=scales_all[quadrant].rearrange("p w (c q j) -> p w c q j", q=4, j=4)[:, :, :, q, :],
             )
 
-        def turn_x(b, r):
-            if r == 0:
-                GX[b] = work.tile([P, 2, 256, 4], BF16, name="gx", align_bytes=64, bufs=8)
-            bank = psum.tile([P, 2, 2, P], F32, name="xtb")
-            words = X[b][:, r, :].bitcast(F32)
-            for h in range(2):
-                for u in range(2):
-                    nc.tensor.transpose(bank[:, h, u, :], words[:, 256 * h + u : 256 * (h + 1) : 2], ident[:])
-            nc.scalar.copy(
-                out=GX[b][:, :, 128 * r : 128 * r + 128, :].bitcast(F32), in_=bank[:].rearrange("p h u n -> p h n u")
-            )
+        w1_wide = keep.tile([P, 2, 4, R], BF16, name="w1_wide", align_bytes=64)
+        w1_laced = keep.tile([P, 2, 4, P, 4], BF16, name="w1_laced", align_bytes=64)
+        w1_codes = keep.tile([P, 2, R], U32, name="w1_codes", align_bytes=64)
+        w1_scales = keep.tile([P, 2, R], U8, name="w1_scales", align_bytes=64)
+        w2_wide = keep.tile([P, 2, 4, R], BF16, name="w2_wide", align_bytes=64)
+        w2_scaled = keep.tile([P, 2, 4, R], BF16, name="w2_scaled", align_bytes=64)
+        w2_laced = keep.tile([P, 2, 4, P, 4], BF16, name="w2_laced", align_bytes=64)
+        w2_codes = keep.tile([P, 2, R], U32, name="w2_codes", align_bytes=64)
+        w2_scales = keep.tile([P, 2, R], U8, name="w2_scales", align_bytes=64)
 
-        def quantize_x(b):
-            XC[b] = work.tile([P, 2, 256], U32, name="xc", align_bytes=64)
-            XS[b] = work.tile([P, 2, 256], U8, name="xs", align_bytes=64)
-            nc.vector.quantize_mx(
-                out=XC[b][:].rearrange("p h n -> p (h n)").bitcast(X4),
-                scales=XS[b][:].rearrange("p h n -> p (h n)"),
-                in_=GX[b][:].rearrange("p h n t -> p (h n t)"),
-            )
+        def widen(copy, wide, raw, c):
+            copy(out=wide[:, c, :, :].rearrange("p t n -> p (t n)"), in_=raw[:, c, :].bitcast(E4M3))
 
-        w1c = keep.tile([P, 2, 512], U32, name="w1c", align_bytes=64)
-        w1s = keep.tile([P, 2, 512], U8, name="w1s", align_bytes=64)
-        w2c = keep.tile([P, 2, 512], U32, name="w2c", align_bytes=64)
-        w2s = keep.tile([P, 2, 512], U8, name="w2s", align_bytes=64)
-        wide1 = keep.tile([P, 2, 4, 512], BF16, name="wide1", align_bytes=64)
-        wide2 = keep.tile([P, 2, 4, 512], BF16, name="wide2", align_bytes=64)
-        grp1 = keep.tile([P, 2, 4, P, 4], BF16, name="grp1", align_bytes=64)
-        ws2 = keep.tile([P, 2, 4, 512], BF16, name="ws2", align_bytes=64)
-        grp2 = keep.tile([P, 2, 4, P, 4], BF16, name="grp2", align_bytes=64)
-
-        def widen(eng, wide, byt, h):
-            o_ = wide[:, h, :, :].rearrange("p t n -> p (t n)")
-            i_ = byt[:, h, :].bitcast(E4M3)
-            if eng == "V":
-                nc.vector.tensor_copy(out=o_, in_=i_)
-            elif eng == "G":
-                nc.gpsimd.tensor_copy(out=o_, in_=i_)
+        def lace_w1(c, j, on_scalar):
+            out_ = w1_laced[:, c, :, 32 * j : 32 * j + 32, :]
+            in_ = w1_wide[:, c, :, 128 * j : 128 * j + 128].rearrange("p t (m u) -> p u m t", u=4)
+            scale = scale_cols[:, 0, c, j : j + 1]
+            if on_scalar:
+                nc.scalar.activation(out=out_, in_=in_, func=ACT.Copy, scale=scale)
             else:
-                nc.scalar.copy(out=o_, in_=i_)
+                nc.vector.tensor_scalar(out=out_, in0=in_, scalar1=scale, scalar2=None, op0=ALU.mult)
 
-        def group_w1(eng, h, j):
-            o_ = grp1[:, h, :, 32 * j : 32 * j + 32, :]
-            i_ = wide1[:, h, :, 128 * j : 128 * j + 128].rearrange("p t (m u) -> p u m t", u=4)
-            if eng == "V":
-                nc.vector.tensor_scalar(out=o_, in0=i_, scalar1=s[:, 0, h, j : j + 1], scalar2=None, op0=ALU.mult)
-            else:
-                nc.scalar.activation(out=o_, in_=i_, func=ACT.Copy, scale=s[:, 0, h, j : j + 1])
-
-        def quantize_w(codes, scales, grp, h):
-            nc.vector.quantize_mx(
-                out=codes[:, h, :].bitcast(X4), scales=scales[:, h, :], in_=grp[:, h].rearrange("p u m t -> p (u m t)")
-            )
-
-        dg = keep.tile([P, 8, P], BF16, name="dg", align_bytes=64)
-        gt32 = keep.tile([P, 8], F32, name="gt32")
-
-        def make_dg():
-            nc.scalar.copy(out=gt32[:], in_=gt[:].rearrange("p h t -> p (h t)"))
-            for i in range(8):
-                nc.scalar.activation(out=dg[:, i, :], in_=ident[:], func=ACT.Copy, scale=gt32[:, i : i + 1])
-
-        def scale_w2_s(h):
-            for t in range(4):
-                for j in range(4):
-                    c = 512 * t + 128 * j
-                    nc.scalar.activation(
-                        out=ws2[:, h, t, 128 * j : 128 * j + 128],
-                        in_=b2[:, h, c : c + 128].bitcast(E4M3),
-                        func=ACT.Copy,
-                        scale=s[:, 1, h, j : j + 1],
-                    )
-
-        def scale_w2(h):
+        def scale_w2(c):
             for j in range(4):
+                columns = slice(128 * j, 128 * j + 128)
                 nc.vector.tensor_scalar(
-                    out=ws2[:, h, :, 128 * j : 128 * j + 128],
-                    in0=wide2[:, h, :, 128 * j : 128 * j + 128],
-                    scalar1=s[:, 1, h, j : j + 1],
+                    out=w2_scaled[:, c, :, columns],
+                    in0=w2_wide[:, c, :, columns],
+                    scalar1=scale_cols[:, 1, c, j : j + 1],
                     scalar2=None,
                     op0=ALU.mult,
                 )
 
-        def turn_w2(h):
-            for tt in range(2):
-                bank = psum.tile([P, 2, 2, P], F32, name="w2b", tag="xtb")
+        def turn_w2(c):
+            for half in range(2):
+                bank = psum.tile([P, 2, 2, P], F32, name="w2_bank", tag="x_turned")
                 for t in range(2):
-                    words = ws2[:, h, 2 * tt + t, :].bitcast(F32)
+                    words = w2_scaled[:, c, 2 * half + t, :].bitcast(F32)
                     for u in range(2):
                         nc.tensor.transpose(bank[:, t, u, :], words[:, u::2], ident[:])
                 nc.scalar.copy(
-                    out=grp2[:, h, 2 * tt : 2 * tt + 2, :, :].bitcast(F32), in_=bank[:].rearrange("p t u m -> p t m u")
+                    out=w2_laced[:, c, 2 * half : 2 * half + 2, :, :].bitcast(F32),
+                    in_=bank[:].rearrange("p t u m -> p t m u"),
                 )
 
+        def quantize_w(codes, scales, laced, c):
+            nc.vector.quantize_mx(
+                out=codes[:, c, :].bitcast(X4),
+                scales=scales[:, c, :],
+                in_=laced[:, c].rearrange("p u m t -> p (u m t)"),
+            )
+
+        def turn_x(b, r):
+            if r == 0:
+                x_laced[b] = work.tile([P, 2, 256, 4], BF16, name="x_laced_tile", align_bytes=64, bufs=8)
+            bank = psum.tile([P, 2, 2, P], F32, name="x_bank", tag="x_turned")
+            words = x_raw[b][:, r, :].bitcast(F32)
+            for c in range(2):
+                for u in range(2):
+                    nc.tensor.transpose(bank[:, c, u, :], words[:, 256 * c + u : 256 * (c + 1) : 2], ident[:])
+            nc.scalar.copy(
+                out=x_laced[b][:, :, 128 * r : 128 * r + 128, :].bitcast(F32),
+                in_=bank[:].rearrange("p c u n -> p c n u"),
+            )
+
+        def quantize_x(b):
+            x_codes[b] = work.tile([P, 2, 256], U32, name="x_codes_tile", align_bytes=64)
+            x_scales[b] = work.tile([P, 2, 256], U8, name="x_scales_tile", align_bytes=64)
+            nc.vector.quantize_mx(
+                out=x_codes[b][:].rearrange("p c n -> p (c n)").bitcast(X4),
+                scales=x_scales[b][:].rearrange("p c n -> p (c n)"),
+                in_=x_laced[b][:].rearrange("p c n t -> p (c n t)"),
+            )
+
         def first_product(b, r):
-            hb = psum.tile([P, 4, P], F32, name="hb")
-            cols = slice(128 * r, 128 * r + 128)
+            bank = psum.tile([P, 4, P], F32, name="h_bank", tag="h_sums")
+            tokens = slice(128 * r, 128 * r + 128)
             for u in range(4):
-                for h in range(2):
-                    wc = slice(128 * u, 128 * u + 128)
+                columns = slice(128 * u, 128 * u + 128)
+                for c in range(2):
                     nc.tensor.matmul_mx(
-                        out=hb[:, u, :],
-                        lhsT=w1c[:, h, wc].bitcast(X4),
-                        lhsT_scale=w1s[:, h, wc],
-                        rhs=XC[b][:, h, cols].bitcast(X4),
-                        rhs_scale=XS[b][:, h, cols],
-                        start=(h == 0),
-                        stop=(h == 1),
+                        out=bank[:, u, :],
+                        lhsT=w1_codes[:, c, columns].bitcast(X4),
+                        lhsT_scale=w1_scales[:, c, columns],
+                        rhs=x_codes[b][:, c, tokens].bitcast(X4),
+                        rhs_scale=x_scales[b][:, c, tokens],
+                        start=(c == 0),
+                        stop=(c == 1),
                     )
-            HB[b, r] = hb
+            h_sums[b, r] = bank
 
         def weigh(b, r):
             if r == 0:
-                HG[b] = work.tile([P, 2, P, 4], BF16, name="hg", align_bytes=64)
+                h_laced[b] = work.tile([P, 2, P, 4], BF16, name="h_laced_tile", align_bytes=64)
             nc.vector.tensor_tensor(
-                out=HG[b][:, r, :, :],
-                in0=HB[b, r][:].rearrange("p u n -> p n u"),
-                in1=a4[:].unsqueeze(1).to_broadcast([P, P, 4]),
+                out=h_laced[b][:, r, :, :],
+                in0=h_sums[b, r][:].rearrange("p u n -> p n u"),
+                in1=a_cols[:].unsqueeze(1).to_broadcast([P, P, 4]),
                 op=ALU.mult,
             )
 
         def quantize_h(b):
-            HC[b] = work.tile([P, 256], U32, name="hc", align_bytes=64, bufs=4)
-            HS[b] = work.tile([P, 256], U8, name="hs", align_bytes=64, bufs=4)
-            nc.vector.quantize_mx(out=HC[b][:].bitcast(X4), scales=HS[b][:], in_=HG[b][:].rearrange("p r n t -> p (r n t)"))
+            h_codes[b] = work.tile([P, 256], U32, name="h_codes_tile", align_bytes=64, bufs=4)
+            h_scales[b] = work.tile([P, 256], U8, name="h_scales_tile", align_bytes=64, bufs=4)
+            nc.vector.quantize_mx(
+                out=h_codes[b][:].bitcast(X4),
+                scales=h_scales[b][:],
+                in_=h_laced[b][:].rearrange("p r n t -> p (r n t)"),
+            )
 
-        def second_product(b, part):
-            tag = "ya" if KIND[b] == "D" else "yb"
-            Y[b, part] = []
+        def result_of(b):
+            if b not in result:
+                result[b] = work.tile([P, 2, D], F32, name="result_tile", align_bytes=64, bufs=4)
+            return result[b]
+
+        def standardise(b, r, engine, factors):
+            product = work.tile([P, D], F32, name="xg_tile", align_bytes=64, bufs=2)
+            engine.tensor_tensor(out=product[:], in0=x_raw[b][:, r, :], in1=factors[:], op=ALU.mult)
+            xg[b, r] = product
+
+        def product_direct(b, r):
+            tokens = slice(128 * r, 128 * r + 128)
+            for c in range(2):
+                bank = psum.tile([P, 4, P], F32, name="y_bank", tag="y_direct")
+                nc.tensor.matmul_mx(
+                    out=bank[:].rearrange("p t m -> p (t m)"),
+                    lhsT=h_codes[b][:, tokens].bitcast(X4),
+                    lhsT_scale=h_scales[b][:, tokens],
+                    rhs=w2_codes[:, c, :].bitcast(X4),
+                    rhs_scale=w2_scales[:, c, :],
+                    start=True,
+                    stop=True,
+                )
+                y_sums[b, r, c] = bank
+
+        def subtract_direct(b, r, c):
+            sensors = slice(512 * c, 512 * c + 512)
+            nc.vector.tensor_tensor(
+                out=result_of(b)[:, r, sensors].rearrange("p (m t) -> p m t", t=4),
+                in0=xg[b, r][:, sensors].rearrange("p (m t) -> p m t", t=4),
+                in1=y_sums[b, r, c][:].rearrange("p t m -> p m t"),
+                op=ALU.subtract,
+            )
+
+        def square_and_store(b, r):
+            tile = result[b][:, r, :]
+            if (b, r) != (PAIRS - 1, 1):
+                nc.scalar.activation(out=tile, in_=tile, func=ACT.Square)
+                nc.sync.dma_start(out=out_pairs[b][:, r, :], in_=tile)
+                return
+            nc.scalar.activation(out=tile[:, 0:512], in_=tile[:, 0:512], func=ACT.Square)
+            nc.sync.dma_start(out=out_pairs[b][:, r, 0:512], in_=tile[:, 0:512])
+            nc.vector.tensor_tensor(out=tile[:, 512:], in0=tile[:, 512:], in1=tile[:, 512:], op=ALU.mult)
+            nc.sync.dma_start(out=out_pairs[b][:, r, 512:], in_=tile[:, 512:])
+
+        def product_turned(b, c):
             for i in range(2):
-                yb = psum.tile([P, 512], F32, name="y", tag=tag)
-                if KIND[b] != "D":
-                    for k in range(2):
-                        wc = slice(256 * i + 128 * k, 256 * i + 128 * k + 128)
-                        nc.tensor.matmul_mx(
-                            out=yb[:, 256 * k : 256 * k + 256],
-                            lhsT=w2c[:, part, wc].bitcast(X4),
-                            lhsT_scale=w2s[:, part, wc],
-                            rhs=HC[b][:].bitcast(X4),
-                            rhs_scale=HS[b][:],
-                            start=True,
-                            stop=True,
-                        )
-                else:
-                    cols = slice(128 * part, 128 * part + 128)
+                bank = psum.tile([P, 2, 256], F32, name="yt_bank", tag="y_turned")
+                for k in range(2):
+                    columns = slice(128 * (2 * i + k), 128 * (2 * i + k) + 128)
                     nc.tensor.matmul_mx(
-                        out=yb[:],
-                        lhsT=HC[b][:, cols].bitcast(X4),
-                        lhsT_scale=HS[b][:, cols],
-                        rhs=w2c[:, i, :].bitcast(X4),
-                        rhs_scale=w2s[:, i, :],
+                        out=bank[:, k, :],
+                        lhsT=w2_codes[:, c, columns].bitcast(X4),
+                        lhsT_scale=w2_scales[:, c, columns],
+                        rhs=h_codes[b][:].bitcast(X4),
+                        rhs_scale=h_scales[b][:],
                         start=True,
                         stop=True,
                     )
-                Y[b, part].append(yb)
+                y_sums[b, c, i] = bank
 
-        def standardise(b, r, eng):
-            xg = work.tile([P, D], F32, name="xg", align_bytes=64, bufs=2)
-            e = nc.gpsimd if eng == "G" else nc.vector
-            e.tensor_tensor(out=xg[:], in0=X[b][:, r, :], in1=(gb if eng == "G" else graw)[:], op=ALU.mult)
-            XGT[b, r] = xg
+        def subtract_turned(b, c, i):
+            if i == 0:
+                turned[b, c] = work.tile([P, 4, 256], F32, name="turned_tile", align_bytes=64, bufs=4)
+            for k in range(2):
+                t = 2 * i + k
+                nc.vector.scalar_tensor_tensor(
+                    out=turned[b, c][:, t, :],
+                    in0=x_laced[b][:, c, :, t],
+                    scalar=g_cols[:, c, t : t + 1],
+                    in1=y_sums[b, c, i][:, k, :],
+                    op0=ALU.mult,
+                    op1=ALU.subtract,
+                )
 
-        def subtract(b, part, halves):
-            if b not in O:
-                O[b] = work.tile([P, 2, D], F32, name="o", align_bytes=64, bufs=4)
-            if KIND[b] == "T" and b + part >= UFROM:
-                if 0 in halves:
-                    ET[b, part] = work.tile([P, 4, 256], F32, name="et", align_bytes=64, bufs=4)
-                for i in halves:
-                    nc.scalar.activation(
-                        out=ET[b, part][:, 2 * i : 2 * i + 2, :].rearrange("p t n -> p (t n)"),
-                        in_=Y[b, part][i][:],
-                        func=ACT.Copy,
-                        scale=-1.0,
-                    )
-            elif KIND[b] == "T":
-                if 0 in halves:
-                    ET[b, part] = work.tile([P, 4, 256], F32, name="et", align_bytes=64, bufs=4)
-                et = ET[b, part]
-                for t in [2 * i + k for i in halves for k in range(2)]:
-                    nc.vector.scalar_tensor_tensor(
-                        out=et[:, t, :],
-                        in0=GX[b][:, part, :, t],
-                        scalar=gt[:, part, t : t + 1],
-                        in1=Y[b, part][t // 2][:, 256 * (t % 2) : 256 * (t % 2) + 256],
-                        op0=ALU.mult,
-                        op1=ALU.subtract,
-                    )
-            else:
-                for h in halves:
-                    c = slice(512 * h, 512 * h + 512)
-                    nc.vector.tensor_tensor(
-                        out=O[b][:, part, c].rearrange("p (m t) -> p m t", t=4),
-                        in0=XGT[b, part][:, c].rearrange("p (m t) -> p m t", t=4),
-                        in1=Y[b, part][h][:].rearrange("p (t m) -> p m t", t=4),
-                        op=ALU.subtract,
-                    )
-
-        def turn_back(b, part, r):
-            et = ET[b, part]
-            ob = psum.tile([P, 4, P], F32, name="ob", tag="yb")
+        def turn_back(b, c, r):
+            bank = psum.tile([P, 4, P], F32, name="back_bank", tag="y_turned")
             for t in range(4):
-                if b + part >= UFROM:
-                    nc.tensor.matmul(
-                        ob[:, t, :],
-                        lhsT=GX[b][:, part, 128 * r : 128 * r + 128, t],
-                        rhs=dg[:, 4 * part + t, :],
-                        start=True,
-                        stop=False,
-                    )
-                    nc.tensor.matmul(
-                        ob[:, t, :],
-                        lhsT=et[:, t, 128 * r : 128 * r + 128],
-                        rhs=ident[:],
-                        is_transpose=True,
-                        start=False,
-                        stop=True,
-                    )
-                else:
-                    nc.tensor.transpose(ob[:, t, :], et[:, t, 128 * r : 128 * r + 128], ident[:])
-            c = slice(512 * part, 512 * part + 512)
+                nc.tensor.transpose(bank[:, t, :], turned[b, c][:, t, 128 * r : 128 * r + 128], ident[:])
+            sensors = slice(512 * c, 512 * c + 512)
             nc.scalar.activation(
-                out=O[b][:, r, c].rearrange("p (m t) -> p m t", t=4),
-                in_=ob[:].rearrange("p t m -> p m t"),
+                out=result_of(b)[:, r, sensors].rearrange("p (m t) -> p m t", t=4),
+                in_=bank[:].rearrange("p t m -> p m t"),
                 func=ACT.Square,
             )
             if r == 1:
-                nc.sync.dma_start(out=ov[b][:, :, c], in_=O[b][:, :, c])
+                nc.sync.dma_start(out=out_pairs[b][:, :, sensors], in_=result[b][:, :, sensors])
 
-        def finish(b, r):
-            if (b, r) == (NP - 1, 1):
-                nc.scalar.activation(out=O[b][:, r, 0:512], in_=O[b][:, r, 0:512], func=ACT.Square)
-                nc.sync.dma_start(out=ov[b][:, r, 0:512], in_=O[b][:, r, 0:512])
-                nc.vector.tensor_tensor(out=O[b][:, r, 512:], in0=O[b][:, r, 512:], in1=O[b][:, r, 512:], op=ALU.mult)
-                nc.sync.dma_start(out=ov[b][:, r, 512:], in_=O[b][:, r, 512:])
-                return
-            nc.scalar.activation(out=O[b][:, r, :], in_=O[b][:, r, :], func=ACT.Square)
-            nc.sync.dma_start(out=ov[b][:, r, :], in_=O[b][:, r, :])
+        def inside(b):
+            return 0 <= b < PAIRS
 
-        def ok(b):
-            return 0 <= b < NP
+        def direct_tile(k):
+            return (2 * (k // 2) + 1, k % 2) if inside(k) else None
 
+        def turned_part(k):
+            return (2 * (k // 2), k % 2) if inside(k) else None
 
-        def tile_of(k):
-            return (2 * (k // 2) + 1, k % 2) if 0 <= k < NP else None
-
-        def part_of(k):
-            return (2 * (k // 2), k % 2) if 0 <= k < NP else None
-
-        widen("S", wide1, b1, 1)
-        for j in range(2, 4):
-            group_w1("S", 1, j)
-        widen("V", wide1, b1, 0)
-        for j in range(2):
-            group_w1("V", 1, j)
+        widen(nc.scalar.copy, w1_wide, w1_raw, 1)
+        for j in (2, 3):
+            lace_w1(1, j, on_scalar=True)
+        widen(nc.vector.tensor_copy, w1_wide, w1_raw, 0)
         turn_x(0, 0)
         turn_x(0, 1)
-        widen("S", wide2, b2, 0)
+        for j in (0, 1):
+            lace_w1(1, j, on_scalar=False)
+        widen(nc.scalar.copy, w2_wide, w2_raw, 0)
         for j in range(4):
-            group_w1("V", 0, j)
+            lace_w1(0, j, on_scalar=False)
         turn_x(1, 0)
-        quantize_w(w1c, w1s, grp1, 1)
-        quantize_w(w1c, w1s, grp1, 0)
-        quantize_x(0)
         turn_x(1, 1)
+        quantize_w(w1_codes, w1_scales, w1_laced, 1)
+        quantize_x(0)
+        widen(nc.scalar.copy, w2_wide, w2_raw, 1)
+        quantize_w(w1_codes, w1_scales, w1_laced, 0)
         scale_w2(0)
-        widen("S", wide2, b2, 1)
-        quantize_x(1)
-        scale_w2(1)
         first_product(0, 0)
         turn_x(2, 0)
+        quantize_x(1)
+        weigh(0, 0)
+        scale_w2(1)
         turn_x(2, 1)
         first_product(0, 1)
-        turn_w2(0)
-        weigh(0, 0)
         weigh(0, 1)
         quantize_x(2)
+        turn_w2(0)
         first_product(1, 0)
-        weigh(1, 0)
+        quantize_h(0)
+        standardise(*direct_tile(0), nc.vector, g_rows)
+        quantize_w(w2_codes, w2_scales, w2_laced, 0)
         turn_w2(1)
         first_product(1, 1)
-        turn_x(3, 0)
+        weigh(1, 0)
         weigh(1, 1)
-        quantize_h(0)
-        turn_x(3, 1)
-        quantize_w(w2c, w2s, grp2, 1)
+        quantize_w(w2_codes, w2_scales, w2_laced, 1)
+        turn_x(3, 0)
         first_product(2, 0)
-        quantize_w(w2c, w2s, grp2, 0)
+        turn_x(3, 1)
         first_product(2, 1)
-        for b in range(NP + 2):
-            dt, pt, nt, old = tile_of(b - 1), part_of(b), tile_of(b), part_of(b - 1)
-            if dt:
-                subtract(*dt, (0,))
-            if old:
-                turn_back(*old, 0)
-            if ok(b + 1):
-                quantize_h(b + 1)
-            if ok(b + 3):
-                quantize_x(b + 3)
-            if ok(b + 8):
-                load_x(b + 8)
-            if old:
-                turn_back(*old, 1)
-            if ok(b + 4):
-                turn_x(b + 4, 0)
-            if b == 0:
-                nc.scalar.copy(out=gb[:], in_=graw[:])
-            if ok(b + 4):
-                turn_x(b + 4, 1)
-            if pt:
-                second_product(*pt)
-            if dt:
-                subtract(*dt, (1,))
-            if nt:
-                second_product(*nt)
-            if nt:
-                standardise(*nt, "V" if b in XGV else "G")
-            if ok(b + 2):
-                weigh(b + 2, 0)
-            if dt:
-                finish(*dt)
-            if ok(b + 3):
-                first_product(b + 3, 0)
-            if ok(b + 2):
-                weigh(b + 2, 1)
-            if ok(b + 3):
-                first_product(b + 3, 1)
-            if pt:
-                subtract(*pt, (0,))
-            if pt:
-                subtract(*pt, (1,))
+
+        for s in range(PAIRS + 1):
+            part, part_before = turned_part(s), turned_part(s - 1)
+            tile, tile_next = direct_tile(s - 1), direct_tile(s)
+            if inside(s + AHEAD):
+                load_x(s + AHEAD)
+            if tile:
+                subtract_direct(*tile, 0)
+            if part_before:
+                turn_back(*part_before, 0)
+            if s == 0:
+                nc.scalar.copy(out=g_rows_late[:], in_=g_rows[:])
+            if part_before:
+                turn_back(*part_before, 1)
+            if inside(s + 4):
+                turn_x(s + 4, 0)
+            if inside(s + 1):
+                quantize_h(s + 1)
+            if inside(s + 3):
+                quantize_x(s + 3)
+            if inside(s + 4):
+                turn_x(s + 4, 1)
+            if part:
+                product_turned(*part)
+            if tile:
+                subtract_direct(*tile, 1)
+            if inside(s + 2):
+                weigh(s + 2, 0)
+            if tile_next:
+                product_direct(*tile_next)
+            if inside(s + 2):
+                weigh(s + 2, 1)
+            if part:
+                subtract_turned(*part, 0)
+            if tile:
+                square_and_store(*tile)
+            if part:
+                subtract_turned(*part, 1)
+            if tile_next and s > 0:
+                standardise(*tile_next, nc.gpsimd, g_rows_late)
+            if inside(s + 3):
+                first_product(s + 3, 0)
+                first_product(s + 3, 1)

from contextlib import ExitStack

import concourse.mybir as mybir
from concourse.masks import make_identity

T, D, R = 4096, 1024, 512
FLOPS = 4 * T * D * R

F32 = mybir.dt.float32
BF16 = mybir.dt.bfloat16
U32 = mybir.dt.uint32
U8 = mybir.dt.uint8
E4M3 = mybir.dt.float8_e4m3fn
X4 = mybir.dt.float8_e4m3fn_x4
ALU = mybir.AluOpType
ACT = mybir.ActivationFunctionType

P = 128
PAIRS = T // 256
AHEAD = 8


def tile_sensor_residual_squared_d7_kernel(tc, x, g, a, w1_bytes, w1_scale, w2_bytes, w2_scale, out):
    nc = tc.nc
    x_pairs = x.rearrange("(b p r) d -> b p (r d)", p=P, r=2)
    out_pairs = out.rearrange("(b p r) d -> b p r d", p=P, r=2)

    with ExitStack() as ctx:
        keep = ctx.enter_context(tc.tile_pool(name="keep", bufs=1))
        x_pool = ctx.enter_context(tc.tile_pool(name="x_pool", bufs=AHEAD + 2))
        work = ctx.enter_context(tc.tile_pool(name="work", bufs=3))
        psum = ctx.enter_context(tc.psum_pool(name="psum", bufs=2))
        ctx.enter_context(tc.manual_schedule())

        x_raw, x_laced, x_codes, x_scales = {}, {}, {}, {}
        h_sums, h_laced, h_codes, h_scales = {}, {}, {}, {}
        y_sums, xg, turned, result = {}, {}, {}, {}

        def load_x(b):
            tile = x_pool.tile([P, 2, D], BF16, name="x_tile", align_bytes=64)
            nc.sync.dma_start(out=tile[:].rearrange("p r d -> p (r d)"), in_=x_pairs[b])
            x_raw[b] = tile

        scales_all = keep.tile([P, 2, 32], F32, name="scales_all")
        nc.scalar.dma_start(out=scales_all[:, 0, :], in_=w1_scale.rearrange("i j -> (i j)").partition_broadcast(P))
        w1_raw = keep.tile([P, 2, 4 * R], U8, name="w1_raw", align_bytes=64)
        w2_raw = keep.tile([P, 2, 4 * R], U8, name="w2_raw", align_bytes=64)
        w1_rows = w1_bytes.rearrange("(c p t) n -> p c (t n)", p=P, t=4)
        w2_rows = w2_bytes.rearrange("(c p t) k -> p c (t k)", p=P, t=4)
        for c in range(2):
            nc.sync.dma_start(out=w1_raw[:, c, :], in_=w1_rows[:, c, :])
        nc.scalar.dma_start(out=scales_all[:, 1, :], in_=w2_scale.rearrange("i j -> (i j)").partition_broadcast(P))
        a_cols = keep.tile([P, 4], BF16, name="a_cols")
        nc.scalar.dma_start(out=a_cols[:], in_=a.rearrange("(p t) -> p t", t=4))
        g_cols = keep.tile([P, 2, 4], BF16, name="g_cols")
        nc.scalar.dma_start(out=g_cols[:], in_=g.rearrange("(c p t) -> p c t", p=P, t=4))
        load_x(0)
        for c in range(2):
            nc.sync.dma_start(out=w2_raw[:, c, :], in_=w2_rows[:, c, :])
        for b in range(1, AHEAD):
            load_x(b)
        g_rows = keep.tile([P, D], BF16, name="g_rows", align_bytes=64)
        nc.sync.dma_start(out=g_rows[:], in_=g.partition_broadcast(P))
        g_rows_late = keep.tile([P, D], BF16, name="g_rows_late", align_bytes=64)

        ident = keep.tile([P, P], F32, name="ident", align_bytes=64)
        make_identity(nc, ident[:])

        scale_cols = keep.tile([P, 2, 2, 4], F32, name="scale_cols")
        for q in range(4):
            quadrant = slice(32 * q, 32 * q + 32)
            nc.vector.tensor_copy(
                out=scale_cols[quadrant],
                in_=scales_all[quadrant].rearrange("p w (c q j) -> p w c q j", q=4, j=4)[:, :, :, q, :],
            )

        w1_wide = keep.tile([P, 2, 4, R], BF16, name="w1_wide", align_bytes=64)
        w1_laced = keep.tile([P, 2, 4, P, 4], BF16, name="w1_laced", align_bytes=64)
        w1_codes = keep.tile([P, 2, R], U32, name="w1_codes", align_bytes=64)
        w1_scales = keep.tile([P, 2, R], U8, name="w1_scales", align_bytes=64)
        w2_wide = keep.tile([P, 2, 4, R], BF16, name="w2_wide", align_bytes=64)
        w2_scaled = keep.tile([P, 2, 4, R], BF16, name="w2_scaled", align_bytes=64)
        w2_laced = keep.tile([P, 2, 4, P, 4], BF16, name="w2_laced", align_bytes=64)
        w2_codes = keep.tile([P, 2, R], U32, name="w2_codes", align_bytes=64)
        w2_scales = keep.tile([P, 2, R], U8, name="w2_scales", align_bytes=64)

        def widen(copy, wide, raw, c):
            copy(out=wide[:, c, :, :].rearrange("p t n -> p (t n)"), in_=raw[:, c, :].bitcast(E4M3))

        def lace_w1(c, j, on_scalar):
            out_ = w1_laced[:, c, :, 32 * j : 32 * j + 32, :]
            in_ = w1_wide[:, c, :, 128 * j : 128 * j + 128].rearrange("p t (m u) -> p u m t", u=4)
            scale = scale_cols[:, 0, c, j : j + 1]
            if on_scalar:
                nc.scalar.activation(out=out_, in_=in_, func=ACT.Copy, scale=scale)
            else:
                nc.vector.tensor_scalar(out=out_, in0=in_, scalar1=scale, scalar2=None, op0=ALU.mult)

        def scale_w2(c):
            for j in range(4):
                columns = slice(128 * j, 128 * j + 128)
                nc.vector.tensor_scalar(
                    out=w2_scaled[:, c, :, columns],
                    in0=w2_wide[:, c, :, columns],
                    scalar1=scale_cols[:, 1, c, j : j + 1],
                    scalar2=None,
                    op0=ALU.mult,
                )

        def turn_w2(c):
            for half in range(2):
                bank = psum.tile([P, 2, 2, P], F32, name="w2_bank", tag="x_turned")
                for t in range(2):
                    words = w2_scaled[:, c, 2 * half + t, :].bitcast(F32)
                    for u in range(2):
                        nc.tensor.transpose(bank[:, t, u, :], words[:, u::2], ident[:])
                nc.scalar.copy(
                    out=w2_laced[:, c, 2 * half : 2 * half + 2, :, :].bitcast(F32),
                    in_=bank[:].rearrange("p t u m -> p t m u"),
                )

        def quantize_w(codes, scales, laced, c):
            nc.vector.quantize_mx(
                out=codes[:, c, :].bitcast(X4),
                scales=scales[:, c, :],
                in_=laced[:, c].rearrange("p u m t -> p (u m t)"),
            )

        def turn_x(b, r):
            if r == 0:
                x_laced[b] = work.tile([P, 2, 256, 4], BF16, name="x_laced_tile", align_bytes=64, bufs=8)
            bank = psum.tile([P, 2, 2, P], F32, name="x_bank", tag="x_turned")
            words = x_raw[b][:, r, :].bitcast(F32)
            for c in range(2):
                for u in range(2):
                    nc.tensor.transpose(bank[:, c, u, :], words[:, 256 * c + u : 256 * (c + 1) : 2], ident[:])
            nc.scalar.copy(
                out=x_laced[b][:, :, 128 * r : 128 * r + 128, :].bitcast(F32),
                in_=bank[:].rearrange("p c u n -> p c n u"),
            )

        def quantize_x(b):
            x_codes[b] = work.tile([P, 2, 256], U32, name="x_codes_tile", align_bytes=64)
            x_scales[b] = work.tile([P, 2, 256], U8, name="x_scales_tile", align_bytes=64)
            nc.vector.quantize_mx(
                out=x_codes[b][:].rearrange("p c n -> p (c n)").bitcast(X4),
                scales=x_scales[b][:].rearrange("p c n -> p (c n)"),
                in_=x_laced[b][:].rearrange("p c n t -> p (c n t)"),
            )

        def first_product(b, r):
            bank = psum.tile([P, 4, P], F32, name="h_bank", tag="h_sums")
            tokens = slice(128 * r, 128 * r + 128)
            for u in range(4):
                columns = slice(128 * u, 128 * u + 128)
                for c in range(2):
                    nc.tensor.matmul_mx(
                        out=bank[:, u, :],
                        lhsT=w1_codes[:, c, columns].bitcast(X4),
                        lhsT_scale=w1_scales[:, c, columns],
                        rhs=x_codes[b][:, c, tokens].bitcast(X4),
                        rhs_scale=x_scales[b][:, c, tokens],
                        start=(c == 0),
                        stop=(c == 1),
                    )
            h_sums[b, r] = bank

        def weigh(b, r):
            if r == 0:
                h_laced[b] = work.tile([P, 2, P, 4], BF16, name="h_laced_tile", align_bytes=64)
            nc.vector.tensor_tensor(
                out=h_laced[b][:, r, :, :],
                in0=h_sums[b, r][:].rearrange("p u n -> p n u"),
                in1=a_cols[:].unsqueeze(1).to_broadcast([P, P, 4]),
                op=ALU.mult,
            )

        def quantize_h(b):
            h_codes[b] = work.tile([P, 256], U32, name="h_codes_tile", align_bytes=64, bufs=4)
            h_scales[b] = work.tile([P, 256], U8, name="h_scales_tile", align_bytes=64, bufs=4)
            nc.vector.quantize_mx(
                out=h_codes[b][:].bitcast(X4),
                scales=h_scales[b][:],
                in_=h_laced[b][:].rearrange("p r n t -> p (r n t)"),
            )

        def result_of(b):
            if b not in result:
                result[b] = work.tile([P, 2, D], F32, name="result_tile", align_bytes=64, bufs=4)
            return result[b]

        def standardise(b, r, engine, factors):
            product = work.tile([P, D], F32, name="xg_tile", align_bytes=64, bufs=2)
            engine.tensor_tensor(out=product[:], in0=x_raw[b][:, r, :], in1=factors[:], op=ALU.mult)
            xg[b, r] = product

        def product_direct(b, r):
            tokens = slice(128 * r, 128 * r + 128)
            for c in range(2):
                bank = psum.tile([P, 4, P], F32, name="y_bank", tag="y_direct")
                nc.tensor.matmul_mx(
                    out=bank[:].rearrange("p t m -> p (t m)"),
                    lhsT=h_codes[b][:, tokens].bitcast(X4),
                    lhsT_scale=h_scales[b][:, tokens],
                    rhs=w2_codes[:, c, :].bitcast(X4),
                    rhs_scale=w2_scales[:, c, :],
                    start=True,
                    stop=True,
                )
                y_sums[b, r, c] = bank

        def subtract_direct(b, r, c):
            sensors = slice(512 * c, 512 * c + 512)
            nc.vector.tensor_tensor(
                out=result_of(b)[:, r, sensors].rearrange("p (m t) -> p m t", t=4),
                in0=xg[b, r][:, sensors].rearrange("p (m t) -> p m t", t=4),
                in1=y_sums[b, r, c][:].rearrange("p t m -> p m t"),
                op=ALU.subtract,
            )

        def square_and_store(b, r):
            tile = result[b][:, r, :]
            if (b, r) != (PAIRS - 1, 1):
                nc.scalar.activation(out=tile, in_=tile, func=ACT.Square)
                nc.sync.dma_start(out=out_pairs[b][:, r, :], in_=tile)
                return
            nc.scalar.activation(out=tile[:, 0:512], in_=tile[:, 0:512], func=ACT.Square)
            nc.sync.dma_start(out=out_pairs[b][:, r, 0:512], in_=tile[:, 0:512])
            nc.vector.tensor_tensor(out=tile[:, 512:], in0=tile[:, 512:], in1=tile[:, 512:], op=ALU.mult)
            nc.sync.dma_start(out=out_pairs[b][:, r, 512:], in_=tile[:, 512:])

        def product_turned(b, c):
            for i in range(2):
                bank = psum.tile([P, 2, 256], F32, name="yt_bank", tag="y_turned")
                for k in range(2):
                    columns = slice(128 * (2 * i + k), 128 * (2 * i + k) + 128)
                    nc.tensor.matmul_mx(
                        out=bank[:, k, :],
                        lhsT=w2_codes[:, c, columns].bitcast(X4),
                        lhsT_scale=w2_scales[:, c, columns],
                        rhs=h_codes[b][:].bitcast(X4),
                        rhs_scale=h_scales[b][:],
                        start=True,
                        stop=True,
                    )
                y_sums[b, c, i] = bank

        def subtract_turned(b, c, i):
            if i == 0:
                turned[b, c] = work.tile([P, 4, 256], F32, name="turned_tile", align_bytes=64, bufs=4)
            for k in range(2):
                t = 2 * i + k
                nc.vector.scalar_tensor_tensor(
                    out=turned[b, c][:, t, :],
                    in0=x_laced[b][:, c, :, t],
                    scalar=g_cols[:, c, t : t + 1],
                    in1=y_sums[b, c, i][:, k, :],
                    op0=ALU.mult,
                    op1=ALU.subtract,
                )

        def turn_back(b, c, r):
            bank = psum.tile([P, 4, P], F32, name="back_bank", tag="y_turned")
            for t in range(4):
                nc.tensor.transpose(bank[:, t, :], turned[b, c][:, t, 128 * r : 128 * r + 128], ident[:])
            sensors = slice(512 * c, 512 * c + 512)
            nc.scalar.activation(
                out=result_of(b)[:, r, sensors].rearrange("p (m t) -> p m t", t=4),
                in_=bank[:].rearrange("p t m -> p m t"),
                func=ACT.Square,
            )
            if r == 1:
                nc.sync.dma_start(out=out_pairs[b][:, :, sensors], in_=result[b][:, :, sensors])

        def inside(b):
            return 0 <= b < PAIRS

        def direct_tile(k):
            return (2 * (k // 2) + 1, k % 2) if inside(k) else None

        def turned_part(k):
            return (2 * (k // 2), k % 2) if inside(k) else None

        widen(nc.scalar.copy, w1_wide, w1_raw, 1)
        for j in (2, 3):
            lace_w1(1, j, on_scalar=True)
        widen(nc.vector.tensor_copy, w1_wide, w1_raw, 0)
        turn_x(0, 0)
        turn_x(0, 1)
        for j in (0, 1):
            lace_w1(1, j, on_scalar=False)
        widen(nc.scalar.copy, w2_wide, w2_raw, 0)
        for j in range(4):
            lace_w1(0, j, on_scalar=False)
        turn_x(1, 0)
        turn_x(1, 1)
        quantize_w(w1_codes, w1_scales, w1_laced, 1)
        quantize_x(0)
        widen(nc.scalar.copy, w2_wide, w2_raw, 1)
        quantize_w(w1_codes, w1_scales, w1_laced, 0)
        scale_w2(0)
        first_product(0, 0)
        turn_x(2, 0)
        quantize_x(1)
        weigh(0, 0)
        scale_w2(1)
        turn_x(2, 1)
        first_product(0, 1)
        weigh(0, 1)
        quantize_x(2)
        turn_w2(0)
        first_product(1, 0)
        quantize_h(0)
        standardise(*direct_tile(0), nc.vector, g_rows)
        quantize_w(w2_codes, w2_scales, w2_laced, 0)
        turn_w2(1)
        first_product(1, 1)
        weigh(1, 0)
        weigh(1, 1)
        quantize_w(w2_codes, w2_scales, w2_laced, 1)
        turn_x(3, 0)
        first_product(2, 0)
        turn_x(3, 1)
        first_product(2, 1)

        for s in range(PAIRS + 1):
            part, part_before = turned_part(s), turned_part(s - 1)
            tile, tile_next = direct_tile(s - 1), direct_tile(s)
            if inside(s + AHEAD):
                load_x(s + AHEAD)
            if tile:
                subtract_direct(*tile, 0)
            if part_before:
                turn_back(*part_before, 0)
            if s == 0:
                nc.scalar.copy(out=g_rows_late[:], in_=g_rows[:])
            if part_before:
                turn_back(*part_before, 1)
            if inside(s + 4):
                turn_x(s + 4, 0)
            if inside(s + 1):
                quantize_h(s + 1)
            if inside(s + 3):
                quantize_x(s + 3)
            if inside(s + 4):
                turn_x(s + 4, 1)
            if part:
                product_turned(*part)
            if tile:
                subtract_direct(*tile, 1)
            if inside(s + 2):
                weigh(s + 2, 0)
            if tile_next:
                product_direct(*tile_next)
            if inside(s + 2):
                weigh(s + 2, 1)
            if part:
                subtract_turned(*part, 0)
            if tile:
                square_and_store(*tile)
            if part:
                subtract_turned(*part, 1)
            if tile_next and s > 0:
                standardise(*tile_next, nc.gpsimd, g_rows_late)
            if inside(s + 3):
                first_product(s + 3, 0)
                first_product(s + 3, 1)
